import numpy as np
import ml_dtypes


def mxq(x, axis, fmt="e4m3"):
    dtype, down = {"e4m3": (ml_dtypes.float8_e4m3fn, 7), "e5m2": (ml_dtypes.float8_e5m2, 14)}[fmt]
    v = np.moveaxis(np.asarray(x, np.float32).astype(ml_dtypes.bfloat16).astype(np.float64), axis, -1)
    blocks = v.reshape(v.shape[:-1] + (-1, 32))
    amax = np.abs(blocks).max(-1, keepdims=True)
    byte = np.maximum(np.where(amax > 0, np.frexp(amax)[1] - 1 + 127, 0) - down, 1)
    scale = np.exp2(byte - 127.0)
    codes = (blocks / scale).astype(np.float32).astype(dtype).astype(np.float64)
    return np.moveaxis((codes * scale).reshape(v.shape), -1, axis)


WIDE = False


def mx_kscale(k):
    if not WIDE:
        return np.ones(k)
    levels = np.array([30, -30])
    if k % 512:
        return np.exp2(np.random.permutation(np.resize(levels, k // 32))).repeat(32)
    a = np.empty((k // 512, 16))
    for p in range(k // 512):
        a[p, :8] = np.random.permutation(np.resize(levels, 8))
        for g in range(8):
            far = levels[np.abs(levels - a[p, g]) >= 10]
            a[p, g + 8] = far[np.random.randint(len(far))]
    return np.exp2(a.ravel()).repeat(32)


def f64(x):
    return np.asarray(x).astype(np.float64)


def striped(idx):
    return np.tile(np.asarray(idx).reshape(-1, 16).T, (8, 1)).astype(np.uint16)


def unstriped(offs):
    return offs[:16].T.reshape(-1).astype(np.int64)


E2M1 = np.array([0.0, 0.5, 1.0, 1.5, 2.0, 3.0, 4.0, 6.0, -0.0, -0.5, -1.0, -1.5, -2.0, -3.0, -4.0, -6.0])


def pack_weight(w, fmt):
    k, n = w.shape
    w = f64(np.asarray(w, np.float32).astype(ml_dtypes.bfloat16)).reshape(k // 32, 32, n)
    amax = np.abs(w).max(1)
    if fmt in ("e4m3", "e5m2"):
        byte = np.frexp(amax)[1] - 1 + 127 - (7 if fmt == "e4m3" else 14)
    else:
        mant, ex = np.frexp(amax / 6.0)
        byte = np.where(mant > 0.5, ex, ex - 1) + 127
    byte = np.clip(np.where(amax > 0, byte, 1), 1, 254)
    scaled = (w * np.exp2(127.0 - byte)[:, None, :]).reshape(k, n).astype(np.float32)
    by_word = np.ascontiguousarray(scaled.reshape(k // 512, 128, 4, n).transpose(0, 1, 3, 2))
    if fmt in ("e4m3", "e5m2"):
        words = by_word.astype(ml_dtypes.float8_e4m3fn if fmt == "e4m3" else ml_dtypes.float8_e5m2).view(np.uint8)
    else:
        c = by_word.astype(ml_dtypes.float4_e2m1fn).view(np.uint8) & 0xF
        words = (c[..., 0::2] | (c[..., 1::2] << 4)).reshape(k // 512, 128, 2 * n)
    return np.ascontiguousarray(words), np.ascontiguousarray(byte.astype(np.uint8).reshape(k // 512, 16, n))


def unpack_weight(words, scales, fmt):
    g, _, n = scales.shape
    words = np.ascontiguousarray(words).reshape(g, 128, n, -1)
    if fmt in ("e4m3", "e5m2"):
        vals = words.view(ml_dtypes.float8_e4m3fn if fmt == "e4m3" else ml_dtypes.float8_e5m2).astype(np.float64)
    else:
        nib = np.empty((g, 128, n, 4), np.uint8)
        nib[..., 0::2] = words & 0xF
        nib[..., 1::2] = words >> 4
        vals = E2M1[nib]
    vals = vals * np.repeat(np.exp2(scales.astype(np.float64) - 127.0), 8, axis=1)[..., None]
    return vals.transpose(0, 1, 3, 2).reshape(g * 512, n)


def sgn(shape):
    return np.random.uniform(0.5, 2.0, shape) * np.where(np.random.standard_normal(shape) < 0, -1.0, 1.0)


K, T, J, R, C, O, N, E = 512, 1024, 256, 512, 512, 128, 256, 1024


def setup_inputs():
    n = np.random.standard_normal
    idx = np.random.permutation(T)[:J]
    idx2 = np.random.permutation(C)[:J]
    idx3 = np.random.permutation(C)[:O]
    idx4 = np.random.permutation(C)[:O]
    idx5 = np.random.permutation(J)[:O]
    idx6 = np.random.permutation(T)[:O]
    idx7 = np.random.permutation(E)[:O]
    fk = mx_kscale(K)
    fr = mx_kscale(R)
    xtp = pack_weight(n((K, T)) / fk[:, None], "e5m2")
    wp = pack_weight(n((K, R)) * 1 / np.sqrt(K) * fk[:, None], "e2m1")
    w2p = pack_weight(n((K, R)) * 1 / np.sqrt(K) * fk[:, None], "e4m3")
    wbp = pack_weight(n((R, N)) * 1 / np.sqrt(R) / fr[:, None], "e2m1")
    wsp = pack_weight(n((K, N)) * 1 / np.sqrt(K) * fk[:, None], "e2m1")
    return {
        "xt_words": xtp[0],
        "xt_scales": xtp[1],
        "w_words": wp[0],
        "w_scales": wp[1],
        "w2_words": w2p[0],
        "w2_scales": w2p[1],
        "sa": (sgn((R, 1)) * fr[:, None]).astype(np.float32),
        "sb": (np.random.uniform(0.5, 1.6, (R, 1)) * fr[:, None]).astype(np.float32),
        "wb_words": wbp[0],
        "wb_scales": wbp[1],
        "ws_words": wsp[0],
        "ws_scales": wsp[1],
        "offs": striped(idx),
        "offs2": striped(idx2),
        "offs3": striped(idx3),
        "offs4": striped(idx4),
        "offs5": striped(idx5),
        "offs6": striped(idx6),
        "offs7": striped(idx7),
    }


def reference(xt_words, xt_scales, w_words, w_scales, w2_words, w2_scales, sa, sb, wb_words, wb_scales, ws_words, ws_scales, offs, offs2, offs3, offs4, offs5, offs6, offs7):
    idx = unstriped(offs)
    idx2 = unstriped(offs2)
    idx3 = unstriped(offs3)
    idx4 = unstriped(offs4)
    idx5 = unstriped(offs5)
    idx6 = unstriped(offs6)
    idx7 = unstriped(offs7)
    xtu = unpack_weight(xt_words, xt_scales, "e5m2")
    wu = unpack_weight(w_words, w_scales, "e2m1")
    w2u = unpack_weight(w2_words, w2_scales, "e4m3")
    wbu = unpack_weight(wb_words, wb_scales, "e2m1")
    wsu = unpack_weight(ws_words, ws_scales, "e2m1")
    xtidxg = xtu[:, idx]
    a = wu.T @ xtidxg
    b = w2u.T @ xtidxg
    pw = np.zeros((R, C))
    pw[:, idx2] = a
    nm = -np.max(pw, axis=1, keepdims=True)
    hid = np.maximum(pw[:, idx3] * f64(sa) * np.exp(pw[:, idx4] + nm), b[:, idx5] * f64(sb))
    hidq = mxq(hid, 0, "e4m3")
    xtidx6g = xtu[:, idx6]
    p = wbu.T @ hidq + wsu.T @ xtidx6g
    y = np.zeros((N, E))
    y[:, idx7] = p
    return y

@@ -1,0 +1,177 @@
+from contextlib import ExitStack
+
+import concourse.mybir as mybir
+
+K, T, J, R, C, O, N, E = 512, 1024, 256, 512, 512, 128, 256, 1024
+FLOPS = 2 * (2 * K * R * J + R * N * O + K * N * O)
+
+F32 = mybir.dt.float32
+BF16 = mybir.dt.bfloat16
+I32 = mybir.dt.int32
+U32 = mybir.dt.uint32
+U16 = mybir.dt.uint16
+U8 = mybir.dt.uint8
+E4M3 = mybir.dt.float8_e4m3fn_x4
+E5M2 = mybir.dt.float8_e5m2_x4
+E2M1 = mybir.dt.float4_e2m1fn_x4
+ALU = mybir.AluOpType
+ACT = mybir.ActivationFunctionType
+
+P = 128
+PACK = 4
+QUAD = 32
+
+
+def tile_list_fadedread_twow_further_scattered_kernel(
+    tc, xt_words, xt_scales, w_words, w_scales, w2_words, w2_scales, sa, sb,
+    wb_words, wb_scales, ws_words, ws_scales,
+    offs, offs2, offs3, offs4, offs5, offs6, offs7, out,
+):
+    nc = tc.nc
+    with ExitStack() as ctx:
+        keep = ctx.enter_context(tc.tile_pool(name="keep", bufs=1))
+        psum = ctx.enter_context(tc.psum_pool(name="psum", bufs=1))
+
+        def sbuf(name, cols, dtype, tag=None):
+            return keep.tile([P, cols], dtype, name=name, tag=tag or name, align_bytes=64)
+
+        def load_list(name, src):
+            tile = sbuf(name, src.shape[1], U16)
+            nc.sync.dma_start(tile[:], src)
+            return tile
+
+        def load_plane(name, src, tag=None):
+            plane = sbuf(name, src.shape[2], U8, tag=tag)
+            rows = src[0].bitcast(I32)
+            for q in range(P // QUAD):
+                four = rows[PACK * q : PACK * (q + 1), :].unsqueeze(0).to_broadcast([QUAD // PACK, PACK, rows.shape[1]])
+                nc.sync.dma_start(plane[QUAD * q : QUAD * (q + 1), :].bitcast(I32), four)
+            return plane
+
+        w_plane_raw = sbuf("w_plane_raw", R, U8)
+        nc.vector.memset(w_plane_raw[:].bitcast(I32), 0)
+        boards = [sbuf(f"board{t}", C, F32) for t in range(PACK)]
+        for board in boards:
+            nc.vector.memset(board[:], 0.0)
+
+        l1 = load_list("l1", offs)
+        w_stage = keep.tile([PACK, P // QUAD, R // 4], I32, name="w_stage")
+        nc.scalar.dma_start(w_stage[:], w_scales[0].bitcast(I32).rearrange("(q r) c -> r q c", r=PACK))
+        w_raw = sbuf("w_raw", 2 * R, U8)
+        nc.scalar.dma_start(w_raw[:].bitcast(I32), w_words[0].bitcast(I32))
+        x_words = sbuf("x_words", T, I32)
+        nc.scalar.dma_start(x_words[:], xt_words[0].rearrange("p c b -> p (c b)").bitcast(I32))
+        x_plane = load_plane("x_plane", xt_scales)
+        w2_raw = sbuf("w2_raw", R, I32, tag="page0")
+        nc.sync.dma_start(w2_raw[:], w2_words[0].rearrange("p c b -> p (c b)").bitcast(I32))
+        w2_plane_raw = load_plane("w2_plane_raw", w2_scales, tag="page1")
+        l2 = load_list("l2", offs2)
+        l4 = load_list("l4", offs4)
+        l3 = load_list("l3", offs3)
+        sa_t = sbuf("sa_t", PACK, F32)
+        nc.sync.dma_start(sa_t[:], sa.rearrange("(p t) o -> p (t o)", t=PACK))
+        l5 = load_list("l5", offs5)
+        sb_t = sbuf("sb_t", PACK, F32)
+        nc.sync.dma_start(sb_t[:], sb.rearrange("(p t) o -> p (t o)", t=PACK))
+        l6 = load_list("l6", offs6)
+        ws_w = sbuf("ws_w", 2 * N, U8)
+        nc.sync.dma_start(ws_w[:].bitcast(I32), ws_words[0].bitcast(I32))
+        wb_w = sbuf("wb_w", 2 * N, U8)
+        nc.sync.dma_start(wb_w[:].bitcast(I32), wb_words[0].bitcast(I32))
+        ws_plane = load_plane("ws_plane", ws_scales)
+        wb_plane = load_plane("wb_plane", wb_scales)
+        l7 = load_list("l7", offs7)
+
+        for q in range(P // QUAD):
+            nc.vector.tensor_copy(w_plane_raw[QUAD * q : QUAD * q + PACK, :].bitcast(I32), w_stage[:, q, :])
+        w_plane = sbuf("w_plane", R, U8)
+        nc.vector.tensor_copy(w_plane[:].rearrange("p (t m) -> p t m", t=PACK), w_plane_raw[:].rearrange("p (m t) -> p t m", t=PACK))
+        w_dealt = sbuf("w_dealt", 2 * R, U8)
+        nc.scalar.copy(w_dealt[:].bitcast(U16).rearrange("p (t m) -> p t m", t=PACK), w_raw[:].bitcast(U16).rearrange("p (m t) -> p t m", t=PACK))
+
+        xg_plane = sbuf("xg_plane", J, U8)
+        nc.vector.tensor_copy(xg_plane[:], x_plane[:].indirect(l1[:]))
+        xg_words = sbuf("xg_words", J, U32)
+        nc.vector.tensor_copy(xg_words[:], x_words[:].bitcast(U32).indirect(l1[:]))
+
+        w2_dealt = sbuf("w2_dealt", R, U32)
+        nc.gpsimd.tensor_copy(w2_dealt[:].rearrange("p (t m) -> p t m", t=PACK), w2_raw[:].bitcast(U32).rearrange("p (m t) -> p t m", t=PACK))
+        w2_plane = sbuf("w2_plane", R, U8)
+        nc.gpsimd.tensor_copy(w2_plane[:].rearrange("p (t m) -> p t m", t=PACK), w2_plane_raw[:].rearrange("p (m t) -> p t m", t=PACK))
+
+        a_ps = [psum.tile([P, J], F32, name=f"a_ps{t}") for t in range(PACK)]
+        b_ps = [psum.tile([P, 2, J], F32, name=f"b_ps{u}") for u in range(2)]
+        p_ps = [psum.tile([P, O], F32, name=f"p_ps{h}") for h in range(2)]
+
+        for t in range(PACK):
+            nc.tensor.matmul_mx(out=a_ps[t][:], lhsT=w_dealt[:, 2 * P * t : 2 * P * (t + 1)].bitcast(E2M1), lhsT_scale=w_plane[:, P * t : P * (t + 1)],
+                                rhs=xg_words[:].bitcast(E5M2), rhs_scale=xg_plane[:], start=True, stop=True)
+        for t in range(PACK):
+            nc.tensor.matmul_mx(out=b_ps[t // 2][:, t % 2, :], lhsT=w2_dealt[:, P * t : P * (t + 1)].bitcast(E4M3), lhsT_scale=w2_plane[:, P * t : P * (t + 1)],
+                                rhs=xg_words[:].bitcast(E5M2), rhs_scale=xg_plane[:], start=True, stop=True)
+
+        a_sb = [sbuf(f"a_sb{t}", J, F32) for t in range(PACK)]
+        b_sb = [sbuf(f"b_sb{t}", J, F32) for t in range(PACK)]
+        top = sbuf("top", PACK, F32)
+        nm = sbuf("nm", PACK, F32)
+        second = keep.tile([P, PACK, O], F32, name="second", align_bytes=64)
+        first = keep.tile([P, PACK, O], F32, name="first", align_bytes=64)
+
+        for t in range(PACK):
+            nc.vector.tensor_scalar(a_sb[t][:], a_ps[t][:], 1.0, 0.0, ALU.mult, ALU.max, accum_out=top[:, t : t + 1])
+        nc.scalar.activation(boards[0][:].indirect(l2[:]), a_sb[0][:], ACT.Copy)
+        nc.vector.tensor_scalar_mul(nm[:], top[:], -1.0)
+        for t in range(1, PACK):
+            nc.vector.tensor_copy(boards[t][:].indirect(l2[:]), a_sb[t][:])
+        picked = []
+
+        def fetch_board(t):
+            both = keep.tile([P, 2, O], F32, name=f"picked{t}", tag=f"b_sb{t}" if t else "picked0", align_bytes=64)
+            nc.scalar.activation(both[:, 0, :], boards[t][:].indirect(l4[:]), ACT.Exp, bias=nm[:, t : t + 1])
+            nc.scalar.activation(both[:, 1, :], boards[t][:].indirect(l3[:]), ACT.Copy, scale=sa_t[:, t : t + 1])
+            picked.append(both)
+
+        fetch_board(0)
+        for t in range(PACK):
+            nc.scalar.activation(b_sb[t][:], b_ps[t // 2][:, t % 2, :], ACT.Copy)
+        for t in range(PACK):
+            nc.scalar.activation(second[:, t, :], b_sb[t][:].indirect(l5[:]), ACT.Copy, scale=sb_t[:, t : t + 1])
+        for t in range(1, PACK):
+            fetch_board(t)
+
+        pages = [sbuf(f"page{h}", E, F32) for h in range(2)]
+        for page in pages:
+            nc.gpsimd.memset(page[:], 0.0)
+
+        x6_plane = sbuf("x6_plane", O, U8)
+        nc.vector.tensor_copy(x6_plane[:], x_plane[:].indirect(l6[:]))
+        x6_words = sbuf("x6_words", O, U32)
+        nc.vector.tensor_copy(x6_words[:], x_words[:].bitcast(U32).indirect(l6[:]))
+        for h in range(2):
+            nc.tensor.matmul_mx(out=p_ps[h][:], lhsT=ws_w[:, 2 * P * h : 2 * P * (h + 1)].bitcast(E2M1), lhsT_scale=ws_plane[:, P * h : P * (h + 1)],
+                                rhs=x6_words[:].bitcast(E5M2), rhs_scale=x6_plane[:], start=True, stop=False)
+
+        for t, both in enumerate(picked):
+            nc.vector.tensor_tensor(first[:, t, :], both[:, 1, :], both[:, 0, :], ALU.mult)
+        hid = sbuf("hid", O * PACK, BF16)
+        nc.vector.tensor_tensor(
+            hid[:].rearrange("p (c i t) -> p c t i", i=4, t=PACK),
+            first[:].rearrange("p t (c i) -> p c t i", i=4),
+            second[:].rearrange("p t (c i) -> p c t i", i=4),
+            ALU.max,
+        )
+        hid_words = sbuf("hid_words", O, U32)
+        hid_plane = sbuf("hid_plane", O, U8)
+        nc.vector.quantize_mx(out=hid_words[:].bitcast(E4M3), scales=hid_plane[:], in_=hid[:])
+
+        for h in range(2):
+            nc.tensor.matmul_mx(out=p_ps[h][:], lhsT=wb_w[:, 2 * P * h : 2 * P * (h + 1)].bitcast(E2M1), lhsT_scale=wb_plane[:, P * h : P * (h + 1)],
+                                rhs=hid_words[:].bitcast(E4M3), rhs_scale=hid_plane[:], start=False, stop=True)
+
+        p_sb = [sbuf(f"p_sb{h}", O, F32) for h in range(2)]
+        nc.vector.tensor_copy(p_sb[0][:], p_ps[0][:])
+        nc.vector.tensor_copy(pages[0][:].indirect(l7[:]), p_sb[0][:])
+        nc.sync.dma_start(out[0:P, :], pages[0][:])
+        nc.scalar.activation(p_sb[1][:], p_ps[1][:], ACT.Copy)
+        nc.scalar.activation(pages[1][:].indirect(l7[:]), p_sb[1][:], ACT.Copy)
+        nc.scalar.dma_start(out[P : 2 * P, :], pages[1][:])

@@ -30,6 +30,7 @@ def tile_list_fadedread_twow_further_scattered_kernel(
     nc = tc.nc
     with ExitStack() as ctx:
         keep = ctx.enter_context(tc.tile_pool(name="keep", bufs=1))
+        shared = ctx.enter_context(tc.tile_pool(name="shared", bufs=1))
         psum = ctx.enter_context(tc.psum_pool(name="psum", bufs=1))
 
         def sbuf(name, cols, dtype, tag=None):
@@ -40,31 +41,32 @@ def tile_list_fadedread_twow_further_scattered_kernel(
             nc.sync.dma_start(tile[:], src)
             return tile
 
-        def load_plane(name, src, tag=None):
+        def load_plane(name, src, queues, tag=None):
             plane = sbuf(name, src.shape[2], U8, tag=tag)
             rows = src[0].bitcast(I32)
-            for q in range(P // QUAD):
+            for q, queue in enumerate(queues):
                 four = rows[PACK * q : PACK * (q + 1), :].unsqueeze(0).to_broadcast([QUAD // PACK, PACK, rows.shape[1]])
-                nc.sync.dma_start(plane[QUAD * q : QUAD * (q + 1), :].bitcast(I32), four)
+                queue.dma_start(plane[QUAD * q : QUAD * (q + 1), :].bitcast(I32), four)
             return plane
 
-        w_plane_raw = sbuf("w_plane_raw", R, U8)
+        w_plane_raw = sbuf("w_plane_raw", R, U8, tag="page1")
         nc.vector.memset(w_plane_raw[:].bitcast(I32), 0)
         boards = [sbuf(f"board{t}", C, F32) for t in range(PACK)]
         for board in boards:
             nc.vector.memset(board[:], 0.0)
 
-        l1 = load_list("l1", offs)
+        on_sync = [nc.sync] * 4
         w_stage = keep.tile([PACK, P // QUAD, R // 4], I32, name="w_stage")
-        nc.scalar.dma_start(w_stage[:], w_scales[0].bitcast(I32).rearrange("(q r) c -> r q c", r=PACK))
+        nc.sync.dma_start(w_stage[:], w_scales[0].bitcast(I32).rearrange("(q r) c -> r q c", r=PACK))
+        l1 = load_list("l1", offs)
+        x_plane = load_plane("x_plane", xt_scales, [nc.sync, nc.sync, nc.scalar, nc.scalar])
         w_raw = sbuf("w_raw", 2 * R, U8)
         nc.scalar.dma_start(w_raw[:].bitcast(I32), w_words[0].bitcast(I32))
         x_words = sbuf("x_words", T, I32)
         nc.scalar.dma_start(x_words[:], xt_words[0].rearrange("p c b -> p (c b)").bitcast(I32))
-        x_plane = load_plane("x_plane", xt_scales)
-        w2_raw = sbuf("w2_raw", R, I32, tag="page0")
+        w2_raw = sbuf("w2_raw", R, I32)
         nc.sync.dma_start(w2_raw[:], w2_words[0].rearrange("p c b -> p (c b)").bitcast(I32))
-        w2_plane_raw = load_plane("w2_plane_raw", w2_scales, tag="page1")
+        w2_plane_raw = load_plane("w2_plane_raw", w2_scales, on_sync)
         l2 = load_list("l2", offs2)
         l4 = load_list("l4", offs4)
         l3 = load_list("l3", offs3)
@@ -78,26 +80,27 @@ def tile_list_fadedread_twow_further_scattered_kernel(
         nc.sync.dma_start(ws_w[:].bitcast(I32), ws_words[0].bitcast(I32))
         wb_w = sbuf("wb_w", 2 * N, U8)
         nc.sync.dma_start(wb_w[:].bitcast(I32), wb_words[0].bitcast(I32))
-        ws_plane = load_plane("ws_plane", ws_scales)
-        wb_plane = load_plane("wb_plane", wb_scales)
+        ws_plane = load_plane("ws_plane", ws_scales, on_sync)
+        wb_plane = load_plane("wb_plane", wb_scales, on_sync)
         l7 = load_list("l7", offs7)
 
         for q in range(P // QUAD):
             nc.vector.tensor_copy(w_plane_raw[QUAD * q : QUAD * q + PACK, :].bitcast(I32), w_stage[:, q, :])
+        xg_plane = sbuf("xg_plane", J, U8)
+        nc.vector.tensor_copy(xg_plane[:], x_plane[:].indirect(l1[:]))
         w_plane = sbuf("w_plane", R, U8)
         nc.vector.tensor_copy(w_plane[:].rearrange("p (t m) -> p t m", t=PACK), w_plane_raw[:].rearrange("p (m t) -> p t m", t=PACK))
         w_dealt = sbuf("w_dealt", 2 * R, U8)
         nc.scalar.copy(w_dealt[:].bitcast(U16).rearrange("p (t m) -> p t m", t=PACK), w_raw[:].bitcast(U16).rearrange("p (m t) -> p t m", t=PACK))
 
-        xg_plane = sbuf("xg_plane", J, U8)
-        nc.vector.tensor_copy(xg_plane[:], x_plane[:].indirect(l1[:]))
         xg_words = sbuf("xg_words", J, U32)
         nc.vector.tensor_copy(xg_words[:], x_words[:].bitcast(U32).indirect(l1[:]))
 
-        w2_dealt = sbuf("w2_dealt", R, U32)
-        nc.gpsimd.tensor_copy(w2_dealt[:].rearrange("p (t m) -> p t m", t=PACK), w2_raw[:].bitcast(U32).rearrange("p (m t) -> p t m", t=PACK))
+
         w2_plane = sbuf("w2_plane", R, U8)
         nc.gpsimd.tensor_copy(w2_plane[:].rearrange("p (t m) -> p t m", t=PACK), w2_plane_raw[:].rearrange("p (m t) -> p t m", t=PACK))
+        w2_dealt = sbuf("w2_dealt", R, U32)
+        nc.scalar.copy(w2_dealt[:].rearrange("p (t m) -> p m t", t=PACK), w2_raw[:].bitcast(U32).rearrange("p (m t) -> p m t", t=PACK))
 
         a_ps = [psum.tile([P, J], F32, name=f"a_ps{t}") for t in range(PACK)]
         b_ps = [psum.tile([P, 2, J], F32, name=f"b_ps{u}") for u in range(2)]
@@ -110,7 +113,8 @@ def tile_list_fadedread_twow_further_scattered_kernel(
             nc.tensor.matmul_mx(out=b_ps[t // 2][:, t % 2, :], lhsT=w2_dealt[:, P * t : P * (t + 1)].bitcast(E4M3), lhsT_scale=w2_plane[:, P * t : P * (t + 1)],
                                 rhs=xg_words[:].bitcast(E5M2), rhs_scale=xg_plane[:], start=True, stop=True)
 
-        a_sb = [sbuf(f"a_sb{t}", J, F32) for t in range(PACK)]
+        a_sb = [sbuf(f"a_sb{t}", J, F32)[:] for t in range(PACK - 1)]
+        a_sb.append(shared.tile([P, J], F32, name="a_last", offset=0, align_bytes=64)[:])
         b_sb = [sbuf(f"b_sb{t}", J, F32) for t in range(PACK)]
         top = sbuf("top", PACK, F32)
         nm = sbuf("nm", PACK, F32)
@@ -118,11 +122,11 @@ def tile_list_fadedread_twow_further_scattered_kernel(
         first = keep.tile([P, PACK, O], F32, name="first", align_bytes=64)
 
         for t in range(PACK):
-            nc.vector.tensor_scalar(a_sb[t][:], a_ps[t][:], 1.0, 0.0, ALU.mult, ALU.max, accum_out=top[:, t : t + 1])
-        nc.scalar.activation(boards[0][:].indirect(l2[:]), a_sb[0][:], ACT.Copy)
+            nc.vector.tensor_scalar(a_sb[t], a_ps[t][:], 1.0, 0.0, ALU.mult, ALU.max, accum_out=top[:, t : t + 1])
+        nc.scalar.activation(boards[0][:].indirect(l2[:]), a_sb[0], ACT.Copy)
         nc.vector.tensor_scalar_mul(nm[:], top[:], -1.0)
         for t in range(1, PACK):
-            nc.vector.tensor_copy(boards[t][:].indirect(l2[:]), a_sb[t][:])
+            nc.vector.tensor_copy(boards[t][:].indirect(l2[:]), a_sb[t])
         picked = []
 
         def fetch_board(t):
@@ -139,13 +143,13 @@ def tile_list_fadedread_twow_further_scattered_kernel(
         for t in range(1, PACK):
             fetch_board(t)
 
-        pages = [sbuf(f"page{h}", E, F32) for h in range(2)]
+        pages = [sbuf("page0", E, F32, tag="a_sb0"), sbuf("page1", E, F32)]
         for page in pages:
             nc.gpsimd.memset(page[:], 0.0)
 
-        x6_plane = sbuf("x6_plane", O, U8)
+        x6_plane = shared.tile([P, O], U8, name="x6_plane", offset=4 * O, align_bytes=64)
         nc.vector.tensor_copy(x6_plane[:], x_plane[:].indirect(l6[:]))
-        x6_words = sbuf("x6_words", O, U32)
+        x6_words = shared.tile([P, O], U32, name="x6_words", offset=0, align_bytes=64)
         nc.vector.tensor_copy(x6_words[:], x_words[:].bitcast(U32).indirect(l6[:]))
         for h in range(2):
             nc.tensor.matmul_mx(out=p_ps[h][:], lhsT=ws_w[:, 2 * P * h : 2 * P * (h + 1)].bitcast(E2M1), lhsT_scale=ws_plane[:, P * h : P * (h + 1)],

@@ -20,6 +20,7 @@ ACT = mybir.ActivationFunctionType
 P = 128
 PACK = 4
 QUAD = 32
+H = J // 2
 
 
 def tile_list_fadedread_twow_further_scattered_kernel(
@@ -94,7 +95,8 @@ def tile_list_fadedread_twow_further_scattered_kernel(
         nc.scalar.copy(w_dealt[:].bitcast(U16).rearrange("p (t m) -> p t m", t=PACK), w_raw[:].bitcast(U16).rearrange("p (m t) -> p t m", t=PACK))
 
         xg_words = sbuf("xg_words", J, U32)
-        nc.vector.tensor_copy(xg_words[:], x_words[:].bitcast(U32).indirect(l1[:]))
+        for u in range(2):
+            nc.vector.tensor_copy(xg_words[:, H * u : H * (u + 1)], x_words[:].bitcast(U32).indirect(l1[:, H // 16 * u : H // 16 * (u + 1)]))
 
 
         w2_plane = sbuf("w2_plane", R, U8)
@@ -102,11 +104,14 @@ def tile_list_fadedread_twow_further_scattered_kernel(
         w2_dealt = sbuf("w2_dealt", R, U32)
         nc.scalar.copy(w2_dealt[:].rearrange("p (t m) -> p m t", t=PACK), w2_raw[:].bitcast(U32).rearrange("p (m t) -> p m t", t=PACK))
 
-        a_ps = [psum.tile([P, J], F32, name=f"a_ps{t}") for t in range(PACK)]
+        a0_ps = [psum.tile([P, H], F32, name=f"a0_ps{u}", tag=f"half{u}") for u in range(2)]
+        a_ps = [None] + [psum.tile([P, J], F32, name=f"a_ps{t}") for t in range(1, PACK)]
         b_ps = [psum.tile([P, 2, J], F32, name=f"b_ps{u}") for u in range(2)]
-        p_ps = [psum.tile([P, O], F32, name=f"p_ps{h}") for h in range(2)]
 
-        for t in range(PACK):
+        for u in range(2):
+            nc.tensor.matmul_mx(out=a0_ps[u][:], lhsT=w_dealt[:, : 2 * P].bitcast(E2M1), lhsT_scale=w_plane[:, :P],
+                                rhs=xg_words[:, H * u : H * (u + 1)].bitcast(E5M2), rhs_scale=xg_plane[:, H * u : H * (u + 1)], start=True, stop=True)
+        for t in range(1, PACK):
             nc.tensor.matmul_mx(out=a_ps[t][:], lhsT=w_dealt[:, 2 * P * t : 2 * P * (t + 1)].bitcast(E2M1), lhsT_scale=w_plane[:, P * t : P * (t + 1)],
                                 rhs=xg_words[:].bitcast(E5M2), rhs_scale=xg_plane[:], start=True, stop=True)
         for t in range(PACK):
@@ -121,9 +126,13 @@ def tile_list_fadedread_twow_further_scattered_kernel(
         second = keep.tile([P, PACK, O], F32, name="second", align_bytes=64)
         first = keep.tile([P, PACK, O], F32, name="first", align_bytes=64)
 
-        for t in range(PACK):
+        half_top = sbuf("half_top", 1, F32)
+        nc.vector.tensor_scalar(a_sb[0][:, :H], a0_ps[0][:], 1.0, 0.0, ALU.mult, ALU.max, accum_out=half_top[:])
+        nc.vector.tensor_scalar(a_sb[0][:, H:], a0_ps[1][:], 1.0, half_top[:], ALU.mult, ALU.max, accum_out=top[:, 0:1])
+        for t in range(1, PACK):
             nc.vector.tensor_scalar(a_sb[t], a_ps[t][:], 1.0, 0.0, ALU.mult, ALU.max, accum_out=top[:, t : t + 1])
-        nc.scalar.activation(boards[0][:].indirect(l2[:]), a_sb[0], ACT.Copy)
+        for u in range(2):
+            nc.scalar.activation(boards[0][:].indirect(l2[:, H // 16 * u : H // 16 * (u + 1)]), a_sb[0][:, H * u : H * (u + 1)], ACT.Copy)
         nc.vector.tensor_scalar_mul(nm[:], top[:], -1.0)
         for t in range(1, PACK):
             nc.vector.tensor_copy(boards[t][:].indirect(l2[:]), a_sb[t])
@@ -147,6 +156,7 @@ def tile_list_fadedread_twow_further_scattered_kernel(
         for page in pages:
             nc.gpsimd.memset(page[:], 0.0)
 
+        p_ps = [psum.tile([P, O], F32, name=f"p_ps{h}", tag=f"half{h}") for h in range(2)]
         x6_plane = shared.tile([P, O], U8, name="x6_plane", offset=4 * O, align_bytes=64)
         nc.vector.tensor_copy(x6_plane[:], x_plane[:].indirect(l6[:]))
         x6_words = shared.tile([P, O], U32, name="x6_words", offset=0, align_bytes=64)
@@ -156,7 +166,8 @@ def tile_list_fadedread_twow_further_scattered_kernel(
                                 rhs=x6_words[:].bitcast(E5M2), rhs_scale=x6_plane[:], start=True, stop=False)
 
         for t, both in enumerate(picked):
-            nc.vector.tensor_tensor(first[:, t, :], both[:, 1, :], both[:, 0, :], ALU.mult)
+            engine = nc.vector if t == PACK - 1 else nc.gpsimd
+            engine.tensor_tensor(first[:, t, :], both[:, 1, :], both[:, 0, :], ALU.mult)
         hid = sbuf("hid", O * PACK, BF16)
         nc.vector.tensor_tensor(
             hid[:].rearrange("p (c i t) -> p c t i", i=4, t=PACK),

from contextlib import ExitStack

import concourse.mybir as mybir

K, T, J, R, C, O, N, E = 512, 1024, 256, 512, 512, 128, 256, 1024
FLOPS = 2 * (2 * K * R * J + R * N * O + K * N * O)

F32 = mybir.dt.float32
BF16 = mybir.dt.bfloat16
I32 = mybir.dt.int32
U32 = mybir.dt.uint32
U16 = mybir.dt.uint16
U8 = mybir.dt.uint8
E4M3 = mybir.dt.float8_e4m3fn_x4
E5M2 = mybir.dt.float8_e5m2_x4
E2M1 = mybir.dt.float4_e2m1fn_x4
ALU = mybir.AluOpType
ACT = mybir.ActivationFunctionType

P = 128
PACK = 4
QUAD = 32
H = J // 2


def tile_list_fadedread_twow_further_scattered_kernel(
    tc, xt_words, xt_scales, w_words, w_scales, w2_words, w2_scales, sa, sb,
    wb_words, wb_scales, ws_words, ws_scales,
    offs, offs2, offs3, offs4, offs5, offs6, offs7, out,
):
    nc = tc.nc
    with ExitStack() as ctx:
        keep = ctx.enter_context(tc.tile_pool(name="keep", bufs=1))
        shared = ctx.enter_context(tc.tile_pool(name="shared", bufs=1))
        psum = ctx.enter_context(tc.psum_pool(name="psum", bufs=1))

        def sbuf(name, cols, dtype, tag=None):
            return keep.tile([P, cols], dtype, name=name, tag=tag or name, align_bytes=64)

        def load_list(name, src):
            tile = sbuf(name, src.shape[1], U16)
            nc.sync.dma_start(tile[:], src)
            return tile

        def load_plane(name, src, queues, tag=None):
            plane = sbuf(name, src.shape[2], U8, tag=tag)
            rows = src[0].bitcast(I32)
            for q, queue in enumerate(queues):
                four = rows[PACK * q : PACK * (q + 1), :].unsqueeze(0).to_broadcast([QUAD // PACK, PACK, rows.shape[1]])
                queue.dma_start(plane[QUAD * q : QUAD * (q + 1), :].bitcast(I32), four)
            return plane

        w_plane_raw = sbuf("w_plane_raw", R, U8, tag="page1")
        nc.vector.memset(w_plane_raw[:].bitcast(I32), 0)
        boards = [sbuf(f"board{t}", C, F32) for t in range(PACK)]
        for board in boards:
            nc.vector.memset(board[:], 0.0)

        on_sync = [nc.sync] * 4
        w_stage = keep.tile([PACK, P // QUAD, R // 4], I32, name="w_stage")
        nc.sync.dma_start(w_stage[:], w_scales[0].bitcast(I32).rearrange("(q r) c -> r q c", r=PACK))
        l1 = load_list("l1", offs)
        x_plane = load_plane("x_plane", xt_scales, [nc.sync, nc.sync, nc.scalar, nc.scalar])
        w_raw = sbuf("w_raw", 2 * R, U8)
        nc.scalar.dma_start(w_raw[:].bitcast(I32), w_words[0].bitcast(I32))
        x_words = sbuf("x_words", T, I32)
        nc.scalar.dma_start(x_words[:], xt_words[0].rearrange("p c b -> p (c b)").bitcast(I32))
        w2_raw = sbuf("w2_raw", R, I32)
        nc.sync.dma_start(w2_raw[:], w2_words[0].rearrange("p c b -> p (c b)").bitcast(I32))
        w2_plane_raw = load_plane("w2_plane_raw", w2_scales, on_sync)
        l2 = load_list("l2", offs2)
        l4 = load_list("l4", offs4)
        l3 = load_list("l3", offs3)
        sa_t = sbuf("sa_t", PACK, F32)
        nc.sync.dma_start(sa_t[:], sa.rearrange("(p t) o -> p (t o)", t=PACK))
        l5 = load_list("l5", offs5)
        sb_t = sbuf("sb_t", PACK, F32)
        nc.sync.dma_start(sb_t[:], sb.rearrange("(p t) o -> p (t o)", t=PACK))
        l6 = load_list("l6", offs6)
        ws_w = sbuf("ws_w", 2 * N, U8)
        nc.sync.dma_start(ws_w[:].bitcast(I32), ws_words[0].bitcast(I32))
        wb_w = sbuf("wb_w", 2 * N, U8)
        nc.sync.dma_start(wb_w[:].bitcast(I32), wb_words[0].bitcast(I32))
        ws_plane = load_plane("ws_plane", ws_scales, on_sync)
        wb_plane = load_plane("wb_plane", wb_scales, on_sync)
        l7 = load_list("l7", offs7)

        for q in range(P // QUAD):
            nc.vector.tensor_copy(w_plane_raw[QUAD * q : QUAD * q + PACK, :].bitcast(I32), w_stage[:, q, :])
        xg_plane = sbuf("xg_plane", J, U8)
        nc.vector.tensor_copy(xg_plane[:], x_plane[:].indirect(l1[:]))
        w_plane = sbuf("w_plane", R, U8)
        nc.vector.tensor_copy(w_plane[:].rearrange("p (t m) -> p t m", t=PACK), w_plane_raw[:].rearrange("p (m t) -> p t m", t=PACK))
        w_dealt = sbuf("w_dealt", 2 * R, U8)
        nc.scalar.copy(w_dealt[:].bitcast(U16).rearrange("p (t m) -> p t m", t=PACK), w_raw[:].bitcast(U16).rearrange("p (m t) -> p t m", t=PACK))

        xg_words = sbuf("xg_words", J, U32)
        for u in range(2):
            nc.vector.tensor_copy(xg_words[:, H * u : H * (u + 1)], x_words[:].bitcast(U32).indirect(l1[:, H // 16 * u : H // 16 * (u + 1)]))


        w2_plane = sbuf("w2_plane", R, U8)
        nc.gpsimd.tensor_copy(w2_plane[:].rearrange("p (t m) -> p t m", t=PACK), w2_plane_raw[:].rearrange("p (m t) -> p t m", t=PACK))
        w2_dealt = sbuf("w2_dealt", R, U32)
        nc.scalar.copy(w2_dealt[:].rearrange("p (t m) -> p m t", t=PACK), w2_raw[:].bitcast(U32).rearrange("p (m t) -> p m t", t=PACK))

        a0_ps = [psum.tile([P, H], F32, name=f"a0_ps{u}", tag=f"half{u}") for u in range(2)]
        a_ps = [None] + [psum.tile([P, J], F32, name=f"a_ps{t}") for t in range(1, PACK)]
        b_ps = [psum.tile([P, 2, J], F32, name=f"b_ps{u}") for u in range(2)]

        for u in range(2):
            nc.tensor.matmul_mx(out=a0_ps[u][:], lhsT=w_dealt[:, : 2 * P].bitcast(E2M1), lhsT_scale=w_plane[:, :P],
                                rhs=xg_words[:, H * u : H * (u + 1)].bitcast(E5M2), rhs_scale=xg_plane[:, H * u : H * (u + 1)], start=True, stop=True)
        for t in range(1, PACK):
            nc.tensor.matmul_mx(out=a_ps[t][:], lhsT=w_dealt[:, 2 * P * t : 2 * P * (t + 1)].bitcast(E2M1), lhsT_scale=w_plane[:, P * t : P * (t + 1)],
                                rhs=xg_words[:].bitcast(E5M2), rhs_scale=xg_plane[:], start=True, stop=True)
        for t in range(PACK):
            nc.tensor.matmul_mx(out=b_ps[t // 2][:, t % 2, :], lhsT=w2_dealt[:, P * t : P * (t + 1)].bitcast(E4M3), lhsT_scale=w2_plane[:, P * t : P * (t + 1)],
                                rhs=xg_words[:].bitcast(E5M2), rhs_scale=xg_plane[:], start=True, stop=True)

        a_sb = [sbuf(f"a_sb{t}", J, F32)[:] for t in range(PACK - 1)]
        a_sb.append(shared.tile([P, J], F32, name="a_last", offset=0, align_bytes=64)[:])
        b_sb = [sbuf(f"b_sb{t}", J, F32) for t in range(PACK)]
        top = sbuf("top", PACK, F32)
        nm = sbuf("nm", PACK, F32)
        second = keep.tile([P, PACK, O], F32, name="second", align_bytes=64)
        first = keep.tile([P, PACK, O], F32, name="first", align_bytes=64)

        half_top = sbuf("half_top", 1, F32)
        nc.vector.tensor_scalar(a_sb[0][:, :H], a0_ps[0][:], 1.0, 0.0, ALU.mult, ALU.max, accum_out=half_top[:])
        nc.vector.tensor_scalar(a_sb[0][:, H:], a0_ps[1][:], 1.0, half_top[:], ALU.mult, ALU.max, accum_out=top[:, 0:1])
        for t in range(1, PACK):
            nc.vector.tensor_scalar(a_sb[t], a_ps[t][:], 1.0, 0.0, ALU.mult, ALU.max, accum_out=top[:, t : t + 1])
        for u in range(2):
            nc.scalar.activation(boards[0][:].indirect(l2[:, H // 16 * u : H // 16 * (u + 1)]), a_sb[0][:, H * u : H * (u + 1)], ACT.Copy)
        nc.vector.tensor_scalar_mul(nm[:], top[:], -1.0)
        for t in range(1, PACK):
            nc.vector.tensor_copy(boards[t][:].indirect(l2[:]), a_sb[t])
        picked = []

        def fetch_board(t):
            both = keep.tile([P, 2, O], F32, name=f"picked{t}", tag=f"b_sb{t}" if t else "picked0", align_bytes=64)
            nc.scalar.activation(both[:, 0, :], boards[t][:].indirect(l4[:]), ACT.Exp, bias=nm[:, t : t + 1])
            nc.scalar.activation(both[:, 1, :], boards[t][:].indirect(l3[:]), ACT.Copy, scale=sa_t[:, t : t + 1])
            picked.append(both)

        fetch_board(0)
        for t in range(PACK):
            nc.scalar.activation(b_sb[t][:], b_ps[t // 2][:, t % 2, :], ACT.Copy)
        for t in range(PACK):
            nc.scalar.activation(second[:, t, :], b_sb[t][:].indirect(l5[:]), ACT.Copy, scale=sb_t[:, t : t + 1])
        for t in range(1, PACK):
            fetch_board(t)

        pages = [sbuf("page0", E, F32, tag="a_sb0"), sbuf("page1", E, F32)]
        for page in pages:
            nc.gpsimd.memset(page[:], 0.0)

        p_ps = [psum.tile([P, O], F32, name=f"p_ps{h}", tag=f"half{h}") for h in range(2)]
        x6_plane = shared.tile([P, O], U8, name="x6_plane", offset=4 * O, align_bytes=64)
        nc.vector.tensor_copy(x6_plane[:], x_plane[:].indirect(l6[:]))
        x6_words = shared.tile([P, O], U32, name="x6_words", offset=0, align_bytes=64)
        nc.vector.tensor_copy(x6_words[:], x_words[:].bitcast(U32).indirect(l6[:]))
        for h in range(2):
            nc.tensor.matmul_mx(out=p_ps[h][:], lhsT=ws_w[:, 2 * P * h : 2 * P * (h + 1)].bitcast(E2M1), lhsT_scale=ws_plane[:, P * h : P * (h + 1)],
                                rhs=x6_words[:].bitcast(E5M2), rhs_scale=x6_plane[:], start=True, stop=False)

        for t, both in enumerate(picked):
            engine = nc.vector if t == PACK - 1 else nc.gpsimd
            engine.tensor_tensor(first[:, t, :], both[:, 1, :], both[:, 0, :], ALU.mult)
        hid = sbuf("hid", O * PACK, BF16)
        nc.vector.tensor_tensor(
            hid[:].rearrange("p (c i t) -> p c t i", i=4, t=PACK),
            first[:].rearrange("p t (c i) -> p c t i", i=4),
            second[:].rearrange("p t (c i) -> p c t i", i=4),
            ALU.max,
        )
        hid_words = sbuf("hid_words", O, U32)
        hid_plane = sbuf("hid_plane", O, U8)
        nc.vector.quantize_mx(out=hid_words[:].bitcast(E4M3), scales=hid_plane[:], in_=hid[:])

        for h in range(2):
            nc.tensor.matmul_mx(out=p_ps[h][:], lhsT=wb_w[:, 2 * P * h : 2 * P * (h + 1)].bitcast(E2M1), lhsT_scale=wb_plane[:, P * h : P * (h + 1)],
                                rhs=hid_words[:].bitcast(E4M3), rhs_scale=hid_plane[:], start=False, stop=True)

        p_sb = [sbuf(f"p_sb{h}", O, F32) for h in range(2)]
        nc.vector.tensor_copy(p_sb[0][:], p_ps[0][:])
        nc.vector.tensor_copy(pages[0][:].indirect(l7[:]), p_sb[0][:])
        nc.sync.dma_start(out[0:P, :], pages[0][:])
        nc.scalar.activation(p_sb[1][:], p_ps[1][:], ACT.Copy)
        nc.scalar.activation(pages[1][:].indirect(l7[:]), p_sb[1][:], ACT.Copy)
        nc.scalar.dma_start(out[P : 2 * P, :], pages[1][:])
